import numpy as np, ml_dtypes
CORES = [33,38,57,62,81,86,161,166,185,190,209,214]
N = 12
import mx_ref
BF = ml_dtypes.bfloat16
def entries(a):
    return np.ascontiguousarray(a.T).reshape(-1)
def table(e):
    return np.ascontiguousarray(np.reshape(e, (-1, 16)).T).astype(np.int32)
def f(rng, *shape):
    return mx_ref.flush((rng.standard_normal(shape, dtype=np.float32) * np.exp2(rng.integers(-2, 3, shape[:-1] + (1,)))).astype(BF))
def wide(rng, *shape, cols=0):
    v = rng.standard_normal(shape, dtype=np.float32) * np.exp2(rng.integers(-12, 13, shape)).astype(np.float32)
    if cols: v *= np.repeat(np.exp2(rng.integers(-cols, cols + 1, shape[:-2] + (1, shape[-1] // 4))) * (rng.random(shape[:-2] + (1, shape[-1] // 4)) > 0.0625), 4, axis=-1).astype(np.float32)
    return mx_ref.flush(v.astype(BF))
NL, LO, O = 1536, 128, 1
HOST = np.array([0 if k < 128 else 1 for k in CORES])
def tables_of(s):
    return np.stack([table(e) for e in s])
def won(rng, win):
    v = rng.integers(1, 2 ** rng.integers(0, 21, NL) + 1)
    s = rng.integers(0, v, (N, NL)); s[win, np.arange(NL)] = v
    return tables_of(s)
def setup_inputs(rng):
    s = rng.integers(0, 2 ** rng.integers(0, 21, NL) + 1, (N, NL))
    return {"x": f(rng, N, 128, 4 * NL), "w": f(rng, N, 128, 512 * O), "sc": tables_of(s)}
def setup_inputs_ties(rng):
    s = np.zeros((N, NL), int)
    for q in range(N):
        for i, j in enumerate(rng.permutation(LO) + q * LO):
            a, b = [rng.permutation(np.flatnonzero(HOST == h)) for h in rng.permutation(2)]
            if i % 3 == 0: e = np.arange(N)
            elif i % 3 == 1: e = a[:rng.integers(2, len(a) + 1)]
            else: e = np.concatenate([a[:rng.integers(1, len(a) + 1)], b[:rng.integers(1, len(b) + 1)]])
            v = 0 if i == 0 else 2 ** 20 if i < 4 else int(rng.integers(1, 2 ** 20 + 1))
            s[:, j] = rng.integers(0, max(v, 1), N); s[e, j] = v
    return {**setup_inputs(rng), "sc": tables_of(s)}
def setup_inputs_close(rng):
    v = rng.integers(1, 2 ** rng.integers(0, 21, NL) + 1)
    v.reshape(N, LO)[:, rng.permutation(LO)[:2]] = [1, 2 ** 20]
    win = rng.integers(0, N, NL); second = (win + rng.integers(1, N, NL)) % N
    s = np.where(rng.random((N, NL)) < 0.5, v - 1, rng.integers(0, v, (N, NL)))
    s[second, np.arange(NL)] = v - 1; s[win, np.arange(NL)] = v
    return {**setup_inputs(rng), "sc": tables_of(s)}
def setup_inputs_most(rng):
    p = int(rng.integers(0, N))
    win = (p + rng.integers(1, N, (N, LO))) % N
    for i, q in enumerate(rng.permutation(N)):
        if i == 0: win[q] = p
        elif i > 1: win[q, rng.permutation(LO)[:-(-9 * LO // 10)]] = p
    return {**setup_inputs(rng), "sc": won(rng, win.reshape(-1))}
def setup_inputs_sides(rng):
    win = np.zeros((N, LO), int)
    for h in range(2):
        own = rng.permutation(np.flatnonzero(HOST == h))
        for i, q in enumerate(own):
            win[q] = rng.choice(np.flatnonzero(HOST == (1 - h if i < len(own) // 2 else h)), LO)
    return {**setup_inputs(rng), "sc": won(rng, win.reshape(-1))}
def setup_inputs_spread(rng):
    d = setup_inputs(rng); d["x"] = wide(rng, N, 128, 4 * NL, cols=6); return d
def check_inputs(d):
    b = []
    for r in range(N):
        s = entries(d["sc"][r])
        if s.min() < 0 or s.max() > 2 ** 20: b.append("sc")
    return b
def reference(x, w, sc):
    best = np.stack([entries(e) for e in sc]).argmax(axis=0)
    y = np.zeros((N, 128, O * LO), np.float32)
    for q in range(N):
        M = np.concatenate([x[best[l]][:, 4 * l:4 * l + 4] for l in range(q * LO, q * LO + LO)], axis=1)
        M = mx_ref.quantize(M)
        for o in range(O): y[q][:, LO * o:LO * o + LO] = mx_ref.matmul(mx_ref.quantize(w[q][:, 512 * o:512 * o + 512]), M)
    return {"y": y}

@@ -1,0 +1,419 @@
+from concourse.bass import DstId, RemoteDMATransfer
+from concourse.mybir import dt, AluOpType, ActivationFunctionType
+
+LO = 128
+LC = 8
+LOW = 8
+
+F8, U8, I32, U16, BF, F32 = "float8_e4m3fn_x4", "uint8", "int32", "uint16", "bfloat16", "float32"
+PAIRS = {"QP": 640, "WP": 768, "XP": 128,
+         "QO": 640, "WO": 1280, "SO": 512,
+         "WF": 512, "MF": 128, "WQ": 128,
+         "RP": 256}
+SCRATCH = {
+    "BP": ("sbuf", [128, 3072], BF), "BO": ("sbuf", [128, 3072], BF), "BW": ("sbuf", [128, 512], BF),
+    "SC": ("sbuf", [128, 96], I32), "KS": ("sbuf", [128, 64], I32), "KP": ("sbuf", [128, 48], I32),
+    "KO": ("sbuf", [128, 48], I32), "KL": ("sbuf", [128, 48], I32), "KW": ("sbuf", [128, 64], I32),
+    "KX": ("sbuf", [128, LC], I32), "RK": ("sbuf", [128, 32], I32), "PM": ("sbuf", [128, LC], I32),
+    "J0": ("sbuf", [128, 40], I32), "J1": ("sbuf", [128, 40], I32), "J2": ("sbuf", [128, 40], I32),
+    "JJ": ("sbuf", [128, 40], I32),
+    "o1": ("sbuf", [128, 40], I32), "o2": ("sbuf", [128, 40], I32), "o3": ("sbuf", [128, 40], I32),
+    "cm": ("sbuf", [128, 48], I32), "ab": ("sbuf", [128, 32], I32), "m1": ("sbuf", [128, LC], I32),
+    "n1": ("sbuf", [128, LC], I32), "om": ("sbuf", [128, LC], I32), "p1": ("sbuf", [128, LC], I32),
+    "p2": ("sbuf", [128, LC], I32), "p3": ("sbuf", [128, LC], I32), "f1": ("sbuf", [128, LC], I32),
+    "f2": ("sbuf", [128, LC], I32), "f3": ("sbuf", [128, LC], I32), "f4": ("sbuf", [128, LC], I32),
+    "f5": ("sbuf", [128, LC], I32), "f6": ("sbuf", [128, LC], I32), "f7": ("sbuf", [128, LC], I32),
+    "lo": ("sbuf", [128, 40], U16), "lp": ("sbuf", [128, LC], U16), "lf": ("sbuf", [128, LC], U16),
+    "ps": ("psum", [128, 512], F32), "ys": ("sbuf", [128, LO], F32),
+}
+for _n, _w in PAIRS.items():
+    SCRATCH[_n + "c"] = ("sbuf", [128, _w], F8)
+    SCRATCH[_n + "s"] = ("sbuf", [128, _w], U8)
+SEMAPHORES = ["xl0", "xl1", "xl2", "xl3", "xl4", "xl5", "wl", "scl", "jot", "kk", "v", "s", "qp0", "qp1", "qp2", "qo", "wq",
+              "kp", "kl", "kx", "pac", "pas", "oec", "oes", "ogc", "ogs", "xxc", "xxs", "hk", "hpc", "hps", "ls",
+              "llo", "llp", "llf", "pm", "pko", "pks", "xpc", "xps", "mfc", "mfs", "mm", "yc", "yst"]
+
+
+def runs(pairs, width):
+    out = []
+    for a, b in pairs:
+        if out and out[-1][0] + out[-1][2] == a and out[-1][1] + out[-1][2] == b:
+            out[-1][2] += width
+        else:
+            out.append([a, b, width])
+    return out
+
+
+def ranks_info(T, topo):
+    cores = [int(c) for c in T.cores]
+    hosts = sorted(set(topo.host(c) for c in cores))
+    by = [[c for c in cores if topo.host(c) == h] for h in hosts]
+    info = {}
+    for h, cs in enumerate(by):
+        groups = []
+        for c in cs:
+            if groups and topo.chip(groups[-1][0]) == topo.chip(c):
+                groups[-1].append(c)
+            else:
+                groups.append([c])
+        for ci, grp in enumerate(groups):
+            able = {}
+            for k, G in enumerate(groups):
+                if k != ci:
+                    able[k] = [c for c in grp if all(topo.may_write(c, d) for d in G)]
+            makes = {c: [] for c in grp}
+            for k in sorted(able, key=lambda k: len(able[k])):
+                c = min(able[k], key=lambda c: len(makes[c]))
+                makes[c] += groups[k]
+            for c in grp:
+                others = [k for k in range(len(groups)) if k != ci]
+                direct = {k: all(topo.may_write(c, d) for d in groups[k]) for k in others}
+                others.sort(key=lambda k: (direct[k], k))
+                relay = {}
+                for k in others:
+                    if not direct[k]:
+                        hs = [m for m in topo.cores_of(c) if m not in cores and topo.die(m) == topo.die(c)
+                              and all(topo.may_write(m, d) for d in groups[k])]
+                        relay[k] = hs[len(relay) % len(hs)]
+                info[c] = {"h": h, "i": cs.index(c), "ci": ci, "groups": groups, "others": others, "relay": relay,
+                           "partner": [d for d in grp if d != c][0], "twin": by[1 - h][cs.index(c)],
+                           "R": makes[c] + [c], "rank": cores.index(c)}
+    return info
+
+
+def key_slot(info, d, s):
+    a = sorted(info[d]["others"]).index(info[s]["ci"])
+    k = info[d]["groups"][info[s]["ci"]].index(s)
+    return 2 * LC * (2 * k + a)
+
+
+def deal(topo, src, dsts, on_only):
+    chip = topo.cores_of(src)
+    off = [d for d in dsts if d not in chip]
+    on = [d for d in dsts if d in chip]
+    pools = {}
+    if off:
+        pools[True] = [e for e in range(16) if all(e in topo.engines(src, d) for d in off)]
+    if on:
+        pools[False] = [e for e in topo.engines(src, on[0]) if e not in (pools.get(True) or on_only)]
+    res, used = [], {True: 0, False: 0}
+    for d in dsts:
+        o = d not in chip
+        n = len(off) if o else len(on)
+        w = 1
+        while 2 * w * n <= len(pools[o]):
+            w *= 2
+        res.append(pools[o][used[o]:used[o] + w])
+        used[o] += w
+    return res
+
+
+def make_calls(T, topo, info):
+    calls = {}
+
+    def add(core, label, transfers, on_only=()):
+        by = {}
+        for t in transfers:
+            by.setdefault(t[5], []).append(t)
+        for w in by:
+            es = deal(topo, core, [t[0] for t in by[w]], on_only)
+            calls.setdefault(core, {}).setdefault(label, []).append([t + (e,) for t, e in zip(by[w], es)])
+
+    for c, f in info.items():
+        p, G = f["partner"], f["groups"]
+        offs = [e for e in topo.engines(c, f["twin"])] if len(f["relay"]) < len(f["others"]) else []
+        tr = []
+        for n, k in enumerate(f["others"]):
+            if k in f["relay"]:
+                hcore = f["relay"][k]
+                tr.append((hcore, "KS", 32 * n, "RK", 0, 32, "hk"))
+                add(hcore, "key", [(d, "RK", 16 * m, "KW", key_slot(info, d, c), 16, "kl") for m, d in enumerate(G[k])])
+            else:
+                tr += [(d, "KS", 32 * n + 16 * m, "KW", key_slot(info, d, c), 16, "kl") for m, d in enumerate(G[k])]
+        tr.append((p, "KP", 0, "KL", 0, LC * (1 + len(info[p]["R"])), "kp"))
+        add(c, "key", tr)
+        for q in "cs":
+            slot = LO * (5 - f["i"])
+            tr = []
+            for n, k in enumerate(f["others"]):
+                if k in f["relay"]:
+                    hcore = f["relay"][k]
+                    tr.append((hcore, "QP" + q, 256 * n, "RP" + q, 0, 256, "hp" + q))
+                    add(hcore, "p" + q, [(d, "RP" + q, LO * m, "WP" + q, slot, LO, "pa" + q) for m, d in enumerate(G[k])])
+            if tr:
+                add(c, "pr" + q, tr)
+            tr = []
+            for n, k in enumerate(f["others"]):
+                if k not in f["relay"]:
+                    tr += [(d, "QP" + q, 256 * n + LO * m, "WP" + q, slot, LO, "pa" + q) for m, d in enumerate(G[k])]
+            tr.append((p, "QP" + q, 512, "WP" + q, slot, LO, "pa" + q))
+            add(c, "pd" + q, tr)
+            nr = len(info[p]["R"])
+            add(c, "oe" + q, [(p, "QO" + q, 0, "WO" + q, LO * nr, LO * nr, "oe" + q)], offs)
+            tr = [(d, "SO" + q, LO * n, "WF" + q, LO * (3 - f["ci"]), LO, "og" + q) for n, d in enumerate(f["R"][:-1])]
+            if tr:
+                add(c, "og" + q, tr)
+            add(c, "xx" + q, [(f["twin"], "XP" + q, 0, "WF" + q, 0, LO, "xx" + q)])
+        add(c, "kx", [(f["twin"], "PM", 0, "KX", 0, LC, "kx")])
+    total = {}
+    for c in calls:
+        for label in calls[c]:
+            for call in calls[c][label]:
+                for t in call:
+                    total[t[0], t[6]] = total.get((t[0], t[6]), 0) + len(t[7])
+                    total[c, "ls"] = total.get((c, "ls"), 0) + len(t[7])
+    return calls, total
+
+
+CACHE = {}
+
+
+def view(T, name, a, w):
+    ap = T[name][:, a:a + w]
+    return ap.bitcast(dt.uint8) if SCRATCH[name][2] == F8 else ap
+
+
+def issue(g, core, T, topo, calls):
+    for call in calls:
+        trs = []
+        for dst, sb, a, db, b, w, sem, eng in call:
+            rid, pid = topo.addr(dst, core)
+            mask = sum(1 << e for e in eng)
+            trs.append((view(T, db, b, w), view(T, sb, a, w), T.sem[sem], rid, pid, mask))
+        if len(trs) == 1:
+            o, i, sem, rid, pid, mask = trs[0]
+            g.remote_dma(o, i, sem, T.sem.ls, pid, rid, mask)
+        else:
+            g.remote_dma_fused([RemoteDMATransfer(dst_ids=[DstId(rid=rid, pnc=pid)], dma_engine_mask=mask, remote_sem=sem,
+                                                  src=i, dst=o) for o, i, sem, rid, pid, mask in trs], local_sem=T.sem.ls)
+
+
+def forward_program(g, core, T, topo, calls, total):
+    for label, sem in (("key", "hk"), ("pc", "hpc"), ("ps", "hps")):
+        g.wait_ge(T.sem[sem], total[core, sem])
+        issue(g, core, T, topo, calls[label])
+    g.wait_ge(T.sem.ls, total[core, "ls"])
+
+
+def rank_program(g, core, T, topo):
+    if "plan" not in CACHE:
+        info = ranks_info(T, topo)
+        CACHE["info"] = info
+        CACHE["plan"] = make_calls(T, topo, info)
+    info, (calls, total) = CACHE["info"], CACHE["plan"]
+    if core not in calls:
+        return
+    if core not in info:
+        forward_program(g, core, T, topo, calls[core], total)
+        return
+    my, f = calls[core], info[core]
+    S, A = T.sem, AluOpType
+    V, ACT = g.vector, g.scalar
+    p, G, R = f["partner"], f["groups"], f["R"]
+    RP = info[p]["R"]
+    nr = len(R)
+    grp = G[f["ci"]]
+    own_o = lambda d: info[d]["rank"]
+    own_p = lambda d: info[info[d]["twin"]]["rank"]
+
+    pchunks = f["others"] + [f["ci"]]
+    ochunks = sorted(range(len(G)), key=lambda k: (0 if any(d in RP for d in G[k] if d != p) else 1 if k == f["ci"] else 2))
+
+    def load_x(q, n):
+        k = (pchunks + ochunks)[n]
+        first = (own_p if n < 3 else own_o)(G[k][0])
+        buf = T.BP if n < 3 else T.BO
+        q.dma_start(buf[:, 1024 * (n % 3):1024 * (n % 3) + 1024], T.x[:, 512 * first:512 * first + 1024]).then_inc(S["xl%d" % n], 16)
+
+    def load_sc(q, t):
+        q.dma_start(T.SC[16 * t:16 * t + 16, :], T.sc[:, :]).then_inc(S.scl, 16)
+
+    load_x(g.sync, 0)
+    for t in range(4):
+        load_sc(ACT, t)
+    for t in range(4, 8):
+        load_sc(g.sync, t)
+    load_x(ACT, 1)
+    load_x(g.sync, 2)
+    for n in range(3, 6):
+        load_x(g.sync, n)
+    g.sync.dma_start(T.BW[:], T.w[:, :]).then_inc(S.wl, 16)
+
+    g.iota(T.J0[:], [[0, 40]], 0, 1).then_inc(S.jot, 1)
+    g.iota(T.J1[:], [[16, 40]], 0, 0).then_inc(S.jot, 1)
+
+    nv = [0]
+
+    def vi(ins):
+        ins.then_inc(S.v, 1)
+        nv[0] += 1
+
+    def vw():
+        V.wait_ge(S.v, nv[0])
+
+    V.wait_ge(S.scl, 128)
+    low = LOW - 1 - f["i"]
+    ks, kp, ko = [], [], []
+    for n, k in enumerate(f["others"]):
+        for m, d in enumerate(G[k]):
+            ks += [(LC * own_p(d), 32 * n + 16 * m), (LC * own_o(d), 32 * n + 16 * m + LC)]
+    kp = [(LC * own_p(p), 0)] + [(LC * own_o(d), LC * (1 + n)) for n, d in enumerate(RP)]
+    ko = [(LC * own_p(core), 0)] + [(LC * own_o(d), LC * (1 + n)) for n, d in enumerate(R)]
+    nk = 0
+    for buf, pairs in ((T.KS, ks), (T.KP, kp)):
+        for a, b, w in runs(pairs, LC):
+            V.tensor_scalar(buf[:, b:b + w], T.SC[:, a:a + w], LOW, low, A.mult, A.add).then_inc(S.kk, 1)
+            nk += 1
+    for a, b, w in runs(ko, LC):
+        vi(V.tensor_scalar(T.KO[:, b:b + w], T.SC[:, a:a + w], LOW, low, A.mult, A.add))
+    V.wait_ge(S.jot, 2)
+    vi(V.tensor_scalar(T.J2[:], T.J0[:], 15, None, A.bitwise_and))
+    vw()
+    vi(V.tensor_tensor(T.JJ[:], T.J2[:], T.J1[:], A.add))
+
+    def quant(dst, b, src, a, cols):
+        return V.quantize_mx(T[dst + "c"][:, b:b + cols], T[dst + "s"][:, b:b + cols], src[:, 4 * a:4 * (a + cols)])
+
+    for n in (0, 1):
+        V.wait_ge(S["xl%d" % n], 16)
+        quant("QP", 256 * n, T.BP, 256 * n, 256).then_inc(S["qp%d" % n], 1)
+    V.wait_ge(S.xl2, 16)
+    quant("QP", 512, T.BP, 512 + LO * grp.index(p), LO).then_inc(S.qp2, 1)
+    vi(quant("WP", LO * (5 - f["i"]), T.BP, 512 + LO * grp.index(core), LO))
+    nqo = 0
+    for n in range(3):
+        V.wait_ge(S["xl%d" % (3 + n)], 16)
+        k = ochunks[n]
+        for lst, dst in ((RP, "QO"), (R, "WO")):
+            for a, b, w in runs([(256 * n + LO * m, LO * lst.index(d)) for m, d in enumerate(G[k]) if d in lst], LO):
+                ins = quant(dst, b, T.BO, a, w)
+                if dst == "QO":
+                    ins.then_inc(S.qo, 1)
+                    nqo += 1
+                else:
+                    vi(ins)
+
+    w8 = LC * nr
+    V.wait_ge(S.kp, total[core, "kp"])
+    vw()
+    vi(V.tensor_tensor(T.o1[:, 0:w8], T.KL[:, LC:LC + w8], T.KO[:, LC:LC + w8], A.is_gt))
+    vi(V.tensor_tensor(T.cm[:, 0:LC + w8], T.KL[:, 0:LC + w8], T.KO[:, 0:LC + w8], A.max))
+    vw()
+    vi(V.tensor_scalar(T.o2[:, 0:w8], T.o1[:, 0:w8], LO * nr, None, A.mult))
+    vw()
+    vi(V.tensor_tensor(T.o3[:, 0:w8], T.o2[:, 0:w8], T.JJ[:, 0:w8], A.add))
+    vw()
+    V.tensor_copy(T.lo[:, 0:w8], T.o3[:, 0:w8]).then_inc(S.llo, 1)
+    V.wait_ge(S.kl, total[core, "kl"])
+    vi(V.tensor_tensor(T.ab[:], T.KW[:, 0:32], T.KW[:, 32:64], A.max))
+    vw()
+    vi(V.tensor_tensor(T.m1[:], T.cm[:, 0:LC], T.ab[:, 0:LC], A.max))
+    vi(V.tensor_tensor(T.n1[:], T.cm[:, w8:LC + w8], T.ab[:, LC:2 * LC], A.max))
+    vw()
+    V.tensor_tensor(T.PM[:], T.m1[:], T.ab[:, 2 * LC:3 * LC], A.max).then_inc(S.pm, 1)
+    vi(V.tensor_tensor(T.om[:], T.n1[:], T.ab[:, 3 * LC:4 * LC], A.max))
+    V.wait_ge(S.pm, 1)
+    vw()
+    vi(V.tensor_scalar(T.p1[:], T.PM[:], LOW - 1, None, A.bitwise_and))
+    vi(V.tensor_scalar(T.f1[:], T.om[:], LOW - 1, 1, A.bitwise_and, A.logical_shift_right))
+    vi(V.tensor_scalar(T.f2[:], T.om[:], 3, None, A.logical_shift_right))
+    vw()
+    vi(V.tensor_scalar(T.p2[:], T.p1[:], LO, -2 * LO, A.mult, A.add))
+    vi(V.tensor_scalar(T.f3[:], T.f1[:], LO, None, A.mult))
+    vw()
+    vi(V.tensor_tensor(T.p3[:], T.p2[:], T.JJ[:, 0:LC], A.add))
+    vw()
+    V.tensor_copy(T.lp[:], T.p3[:]).then_inc(S.llp, 1)
+    V.wait_ge(S.wl, 16)
+    quant("WQ", 0, T.BW, 0, LO).then_inc(S.wq, 1)
+
+    def pick_c(dst, b, src, w, lst, a, k):
+        return V.tensor_copy(T[dst + "c"][:, b:b + LC * 2 * k].bitcast(dt.uint32),
+                             T[src + "c"][:, 0:w].bitcast(dt.uint32).indirect(T[lst][:, a:a + k]))
+
+    def pick_s(dst, b, src, w, lst, a, k):
+        return ACT.activation(T[dst + "s"][:, b:b + LC * 2 * k], T[src + "s"][:, 0:w].indirect(T[lst][:, a:a + k]),
+                              ActivationFunctionType.Copy)
+
+    slot = LO * (3 - f["ci"])
+    V.wait_ge(S.llo, 1)
+    V.wait_ge(S.oec, total[core, "oec"])
+    if nr > 1:
+        pick_c("SO", 0, "WO", 2 * LO * nr, "lo", 0, LC * (nr - 1)).then_inc(S.pko, 1)
+    vi(pick_c("WF", slot, "WO", 2 * LO * nr, "lo", LC * (nr - 1), LC))
+    V.wait_ge(S.llp, 1)
+    V.wait_ge(S.pac, total[core, "pac"])
+    pick_c("XP", 0, "WP", 6 * LO, "lp", 0, LC).then_inc(S.xpc, 1)
+    V.wait_ge(S.kx, total[core, "kx"])
+    vi(V.tensor_scalar(T.f4[:], T.KX[:], 3, None, A.logical_shift_right))
+    vw()
+    vi(V.tensor_tensor(T.f5[:], T.f2[:], T.f4[:], A.is_ge if f["h"] == 0 else A.is_gt))
+    vw()
+    vi(V.tensor_tensor(T.f6[:], T.f5[:], T.f3[:], A.mult))
+    vw()
+    vi(V.tensor_tensor(T.f7[:], T.f6[:], T.JJ[:, 0:LC], A.add))
+    vw()
+    V.tensor_copy(T.lf[:], T.f7[:]).then_inc(S.llf, 1)
+    V.wait_ge(S.llf, 1)
+    V.wait_ge(S.ogc, total[core, "ogc"])
+    V.wait_ge(S.xxc, total[core, "xxc"])
+    pick_c("MF", 0, "WF", 4 * LO, "lf", 0, LC).then_inc(S.mfc, 1)
+    V.wait_ge(S.mm, 1)
+    V.tensor_copy(T.ys[:], T.ps[:, 0:LO]).then_inc(S.yc, 1)
+
+    ns = [0]
+    ACT.wait_ge(S.llo, 1)
+    ACT.wait_ge(S.oes, total[core, "oes"])
+    if nr > 1:
+        pick_s("SO", 0, "WO", 2 * LO * nr, "lo", 0, LC * (nr - 1)).then_inc(S.pks, 1)
+    pick_s("WF", slot, "WO", 2 * LO * nr, "lo", LC * (nr - 1), LC).then_inc(S.s, 1)
+    ACT.wait_ge(S.llp, 1)
+    ACT.wait_ge(S.pas, total[core, "pas"])
+    pick_s("XP", 0, "WP", 6 * LO, "lp", 0, LC).then_inc(S.xps, 1)
+    ACT.wait_ge(S.llf, 1)
+    ACT.wait_ge(S.s, 1)
+    ACT.wait_ge(S.ogs, total[core, "ogs"])
+    ACT.wait_ge(S.xxs, total[core, "xxs"])
+    pick_s("MF", 0, "WF", 4 * LO, "lf", 0, LC).then_inc(S.mfs, 1)
+
+    g.tensor.wait_ge(S.wq, 1)
+    g.tensor.wait_ge(S.mfs, 1)
+    g.tensor.wait_ge(S.mfc, 1)
+    g.tensor.matmul_mx(T.ps[:, 0:LO], T.WQc[:, 0:LO], T.WQs[:, 0:LO], T.MFc[:, 0:LO], T.MFs[:, 0:LO], True, True).then_inc(S.mm, 1)
+    g.sync.wait_ge(S.yc, 1)
+    g.sync.dma_start(T.y[:, :], T.ys[:]).then_inc(S.yst, 16)
+    g.sync.wait_ge(S.yst, 16)
+    V.wait_ge(S.v, nv[0])
+
+    def send(label):
+        issue(g, core, T, topo, my[label])
+
+    g.wait_ge(S.kk, nk)
+    send("key")
+    for n, k in enumerate(f["others"]):
+        if k in f["relay"]:
+            g.wait_ge(S["qp%d" % n], 1)
+    if f["relay"]:
+        send("prc")
+        send("prs")
+    for n, k in enumerate(f["others"]):
+        if k not in f["relay"]:
+            g.wait_ge(S["qp%d" % n], 1)
+    g.wait_ge(S.qp2, 1)
+    send("pdc")
+    send("pds")
+    g.wait_ge(S.qo, nqo)
+    send("oec")
+    send("oes")
+    g.wait_ge(S.pm, 1)
+    send("kx")
+    if nr > 1:
+        g.wait_ge(S.pko, 1)
+        send("ogc")
+        g.wait_ge(S.pks, 1)
+        send("ogs")
+    g.wait_ge(S.xpc, 1)
+    send("xxc")
+    g.wait_ge(S.xps, 1)
+    send("xxs")
+    g.wait_ge(S.ls, total[core, "ls"])

@@ -4,34 +4,35 @@ from concourse.mybir import dt, AluOpType, ActivationFunctionType
 LO = 128
 LC = 8
 LOW = 8
+PO = 512
 
 F8, U8, I32, U16, BF, F32 = "float8_e4m3fn_x4", "uint8", "int32", "uint16", "bfloat16", "float32"
 PAIRS = {"QP": 640, "WP": 768, "XP": 128,
-         "QO": 640, "WO": 1280, "SO": 512,
+         "QO": 640, "WO": 1024, "SO": 384,
          "WF": 512, "MF": 128, "WQ": 128,
-         "RP": 256}
+         "RP": 256, "RO": 128}
 SCRATCH = {
     "BP": ("sbuf", [128, 3072], BF), "BO": ("sbuf", [128, 3072], BF), "BW": ("sbuf", [128, 512], BF),
-    "SC": ("sbuf", [128, 96], I32), "KS": ("sbuf", [128, 64], I32), "KP": ("sbuf", [128, 48], I32),
-    "KO": ("sbuf", [128, 48], I32), "KL": ("sbuf", [128, 48], I32), "KW": ("sbuf", [128, 64], I32),
+    "SC": ("sbuf", [128, 96], I32), "KS": ("sbuf", [128, 64], I32), "KP": ("sbuf", [128, 40], I32),
+    "KO": ("sbuf", [128, 40], I32), "KL": ("sbuf", [128, 40], I32), "KW": ("sbuf", [128, 64], I32),
     "KX": ("sbuf", [128, LC], I32), "RK": ("sbuf", [128, 32], I32), "PM": ("sbuf", [128, LC], I32),
-    "J0": ("sbuf", [128, 40], I32), "J1": ("sbuf", [128, 40], I32), "J2": ("sbuf", [128, 40], I32),
-    "JJ": ("sbuf", [128, 40], I32),
-    "o1": ("sbuf", [128, 40], I32), "o2": ("sbuf", [128, 40], I32), "o3": ("sbuf", [128, 40], I32),
-    "cm": ("sbuf", [128, 48], I32), "ab": ("sbuf", [128, 32], I32), "m1": ("sbuf", [128, LC], I32),
-    "n1": ("sbuf", [128, LC], I32), "om": ("sbuf", [128, LC], I32), "p1": ("sbuf", [128, LC], I32),
-    "p2": ("sbuf", [128, LC], I32), "p3": ("sbuf", [128, LC], I32), "f1": ("sbuf", [128, LC], I32),
-    "f2": ("sbuf", [128, LC], I32), "f3": ("sbuf", [128, LC], I32), "f4": ("sbuf", [128, LC], I32),
-    "f5": ("sbuf", [128, LC], I32), "f6": ("sbuf", [128, LC], I32), "f7": ("sbuf", [128, LC], I32),
-    "lo": ("sbuf", [128, 40], U16), "lp": ("sbuf", [128, LC], U16), "lf": ("sbuf", [128, LC], U16),
+    "J0": ("sbuf", [128, 32], I32), "J1": ("sbuf", [128, 32], I32), "J2": ("sbuf", [128, 32], I32),
+    "JJ": ("sbuf", [128, 32], I32), "JL": ("sbuf", [128, LC], F32), "JO": ("sbuf", [128, 32], F32),
+    "o1": ("sbuf", [128, 32], I32), "o2": ("sbuf", [128, 32], F32),
+    "cm": ("sbuf", [128, 16], I32), "ab": ("sbuf", [128, 32], I32), "m1": ("sbuf", [128, 16], I32),
+    "om": ("sbuf", [128, LC], I32), "p1": ("sbuf", [128, LC], I32), "p2": ("sbuf", [128, LC], F32),
+    "f1": ("sbuf", [128, LC], I32), "f2": ("sbuf", [128, LC], I32), "f3": ("sbuf", [128, LC], I32),
+    "f4": ("sbuf", [128, LC], I32), "f5": ("sbuf", [128, LC], I32), "f6": ("sbuf", [128, LC], I32),
+    "f7": ("sbuf", [128, LC], F32),
+    "lo": ("sbuf", [128, 32], U16), "lp": ("sbuf", [128, LC], U16), "lf": ("sbuf", [128, LC], U16),
     "ps": ("psum", [128, 512], F32), "ys": ("sbuf", [128, LO], F32),
 }
 for _n, _w in PAIRS.items():
     SCRATCH[_n + "c"] = ("sbuf", [128, _w], F8)
     SCRATCH[_n + "s"] = ("sbuf", [128, _w], U8)
-SEMAPHORES = ["xl0", "xl1", "xl2", "xl3", "xl4", "xl5", "wl", "scl", "jot", "kk", "v", "s", "qp0", "qp1", "qp2", "qo", "wq",
-              "kp", "kl", "kx", "pac", "pas", "oec", "oes", "ogc", "ogs", "xxc", "xxs", "hk", "hpc", "hps", "ls",
-              "llo", "llp", "llf", "pm", "pko", "pks", "xpc", "xps", "mfc", "mfs", "mm", "yc", "yst"]
+SEMAPHORES = ["xl0", "xl1", "xl2", "xl3", "xl4", "xl5", "wl", "scl", "jot", "ks", "kk", "v", "s", "qp0", "qp1", "qp2", "qo",
+              "wq", "kp", "kl", "kx", "pac", "pas", "oec", "oes", "ogc", "ogs", "xxc", "xxs", "hk", "hpc", "hps", "hoc",
+              "hos", "ls", "llo", "llp", "llf", "pm", "pko", "pks", "xpc", "xps", "mfc", "mfs", "mm", "yc", "yst"]
 
 
 def runs(pairs, width):
@@ -65,6 +66,8 @@ def ranks_info(T, topo):
             for k in sorted(able, key=lambda k: len(able[k])):
                 c = min(able[k], key=lambda c: len(makes[c]))
                 makes[c] += groups[k]
+            if any(not makes[c] for c in grp):
+                makes = {c: [groups[k][m] for k in sorted(able)] for m, c in enumerate(grp)}
             for c in grp:
                 others = [k for k in range(len(groups)) if k != ci]
                 direct = {k: all(topo.may_write(c, d) for d in groups[k]) for k in others}
@@ -77,7 +80,7 @@ def ranks_info(T, topo):
                         relay[k] = hs[len(relay) % len(hs)]
                 info[c] = {"h": h, "i": cs.index(c), "ci": ci, "groups": groups, "others": others, "relay": relay,
                            "partner": [d for d in grp if d != c][0], "twin": by[1 - h][cs.index(c)],
-                           "R": makes[c] + [c], "rank": cores.index(c)}
+                           "R": [c] + makes[c], "rank": cores.index(c)}
     return info
 
 
@@ -93,7 +96,7 @@ def deal(topo, src, dsts, on_only):
     on = [d for d in dsts if d in chip]
     pools = {}
     if off:
-        pools[True] = [e for e in range(16) if all(e in topo.engines(src, d) for d in off)]
+        pools[True] = [e for e in topo.engines(src, off[0]) if all(e in topo.engines(src, d) for d in off)]
     if on:
         pools[False] = [e for e in topo.engines(src, on[0]) if e not in (pools.get(True) or on_only)]
     res, used = [], {True: 0, False: 0}
@@ -121,17 +124,24 @@ def make_calls(T, topo, info):
 
     for c, f in info.items():
         p, G = f["partner"], f["groups"]
-        offs = [e for e in topo.engines(c, f["twin"])] if len(f["relay"]) < len(f["others"]) else []
-        tr = []
+        nr = len(info[p]["R"])
+        offs = topo.engines(c, f["twin"]) if len(f["relay"]) < len(f["others"]) else []
+        tr, dr = [], []
         for n, k in enumerate(f["others"]):
             if k in f["relay"]:
                 hcore = f["relay"][k]
                 tr.append((hcore, "KS", 32 * n, "RK", 0, 32, "hk"))
                 add(hcore, "key", [(d, "RK", 16 * m, "KW", key_slot(info, d, c), 16, "kl") for m, d in enumerate(G[k])])
             else:
-                tr += [(d, "KS", 32 * n + 16 * m, "KW", key_slot(info, d, c), 16, "kl") for m, d in enumerate(G[k])]
-        tr.append((p, "KP", 0, "KL", 0, LC * (1 + len(info[p]["R"])), "kp"))
-        add(c, "key", tr)
+                dr += [(d, "KS", 32 * n + 16 * m, "KW", key_slot(info, d, c), 16, "kl") for m, d in enumerate(G[k])]
+        kp = [(p, "KP", 0, "KL", 0, LC * (1 + nr), "kp")]
+        if tr:
+            add(c, "k1", tr + kp)
+            if dr:
+                add(c, "k2", dr)
+        else:
+            add(c, "k1", dr)
+            add(c, "k2", kp, offs)
         for q in "cs":
             slot = LO * (5 - f["i"])
             tr = []
@@ -148,11 +158,16 @@ def make_calls(T, topo, info):
                     tr += [(d, "QP" + q, 256 * n + LO * m, "WP" + q, slot, LO, "pa" + q) for m, d in enumerate(G[k])]
             tr.append((p, "QP" + q, 512, "WP" + q, slot, LO, "pa" + q))
             add(c, "pd" + q, tr)
-            nr = len(info[p]["R"])
-            add(c, "oe" + q, [(p, "QO" + q, 0, "WO" + q, LO * nr, LO * nr, "oe" + q)], offs)
-            tr = [(d, "SO" + q, LO * n, "WF" + q, LO * (3 - f["ci"]), LO, "og" + q) for n, d in enumerate(f["R"][:-1])]
-            if tr:
-                add(c, "og" + q, tr)
+            add(c, "oe" + q, [(p, "QO" + q, 0, "WO" + q, PO, LO * nr, "oe" + q)], offs)
+            tr, slot = [], LO * (3 - f["ci"])
+            for n, d in enumerate(f["R"][1:]):
+                hcore = f["relay"].get(info[d]["ci"])
+                if hcore is None:
+                    tr.append((d, "SO" + q, LO * n, "WF" + q, slot, LO, "og" + q))
+                else:
+                    tr.append((hcore, "SO" + q, LO * n, "RO" + q, 0, LO, "ho" + q))
+                    add(hcore, "o" + q, [(d, "RO" + q, 0, "WF" + q, slot, LO, "og" + q)])
+            add(c, "og" + q, tr)
             add(c, "xx" + q, [(f["twin"], "XP" + q, 0, "WF" + q, 0, LO, "xx" + q)])
         add(c, "kx", [(f["twin"], "PM", 0, "KX", 0, LC, "kx")])
     total = {}
@@ -189,17 +204,17 @@ def issue(g, core, T, topo, calls):
 
 
 def forward_program(g, core, T, topo, calls, total):
-    for label, sem in (("key", "hk"), ("pc", "hpc"), ("ps", "hps")):
-        g.wait_ge(T.sem[sem], total[core, sem])
-        issue(g, core, T, topo, calls[label])
+    for label, sem in (("key", "hk"), ("pc", "hpc"), ("ps", "hps"), ("oc", "hoc"), ("os", "hos")):
+        if label in calls:
+            g.wait_ge(T.sem[sem], total[core, sem])
+            issue(g, core, T, topo, calls[label])
     g.wait_ge(T.sem.ls, total[core, "ls"])
 
 
 def rank_program(g, core, T, topo):
     if "plan" not in CACHE:
-        info = ranks_info(T, topo)
-        CACHE["info"] = info
-        CACHE["plan"] = make_calls(T, topo, info)
+        CACHE["info"] = ranks_info(T, topo)
+        CACHE["plan"] = make_calls(T, topo, CACHE["info"])
     info, (calls, total) = CACHE["info"], CACHE["plan"]
     if core not in calls:
         return
@@ -229,18 +244,18 @@ def rank_program(g, core, T, topo):
         q.dma_start(T.SC[16 * t:16 * t + 16, :], T.sc[:, :]).then_inc(S.scl, 16)
 
     load_x(g.sync, 0)
-    for t in range(4):
-        load_sc(ACT, t)
-    for t in range(4, 8):
+    for t in range(5, 8):
         load_sc(g.sync, t)
-    load_x(ACT, 1)
-    load_x(g.sync, 2)
-    for n in range(3, 6):
+    for n in (1, 3, 5):
         load_x(g.sync, n)
+    for t in range(5):
+        load_sc(ACT, t)
+    for n in (2, 4):
+        load_x(ACT, n)
     g.sync.dma_start(T.BW[:], T.w[:, :]).then_inc(S.wl, 16)
 
-    g.iota(T.J0[:], [[0, 40]], 0, 1).then_inc(S.jot, 1)
-    g.iota(T.J1[:], [[16, 40]], 0, 0).then_inc(S.jot, 1)
+    g.iota(T.J0[:], [[0, 32]], 0, 1).then_inc(S.jot, 1)
+    g.iota(T.J1[:], [[16, 32]], 0, 0).then_inc(S.jot, 1)
 
     nv = [0]
 
@@ -253,23 +268,34 @@ def rank_program(g, core, T, topo):
 
     V.wait_ge(S.scl, 128)
     low = LOW - 1 - f["i"]
-    ks, kp, ko = [], [], []
+
+    def key(buf, b, e, step, a, sem):
+        w = len(range(b, e, step))
+        ins = V.tensor_scalar(buf[:, b:e:step], T.SC[:, a:a + w], LOW, low, A.mult, A.add)
+        if sem is None:
+            vi(ins)
+        else:
+            ins.then_inc(sem, 1)
+
     for n, k in enumerate(f["others"]):
-        for m, d in enumerate(G[k]):
-            ks += [(LC * own_p(d), 32 * n + 16 * m), (LC * own_o(d), 32 * n + 16 * m + LC)]
-    kp = [(LC * own_p(p), 0)] + [(LC * own_o(d), LC * (1 + n)) for n, d in enumerate(RP)]
-    ko = [(LC * own_p(core), 0)] + [(LC * own_o(d), LC * (1 + n)) for n, d in enumerate(R)]
-    nk = 0
-    for buf, pairs in ((T.KS, ks), (T.KP, kp)):
-        for a, b, w in runs(pairs, LC):
-            V.tensor_scalar(buf[:, b:b + w], T.SC[:, a:a + w], LOW, low, A.mult, A.add).then_inc(S.kk, 1)
-            nk += 1
-    for a, b, w in runs(ko, LC):
-        vi(V.tensor_scalar(T.KO[:, b:b + w], T.SC[:, a:a + w], LOW, low, A.mult, A.add))
+        b = 4 * LC * n
+        key(T.KS, b, b + 4 * LC, 2, LC * own_p(G[k][0]), S.ks)
+        key(T.KS, b + 1, b + 4 * LC, 2, LC * own_o(G[k][0]), S.ks)
+    npk = 0
+    for buf, lst, sem in ((T.KP, RP, S.kk), (T.KO, R, None)):
+        key(buf, 0, 2 * LC, 2, LC * own_p(lst[0]), sem)
+        key(buf, 1, 2 * LC, 2, LC * own_o(lst[0]), sem)
+        rr = runs([(LC * own_o(d), LC * (1 + n)) for n, d in enumerate(lst) if n], LC)
+        for a, b, w in rr:
+            key(buf, b, b + w, 1, a, sem)
+        npk = npk or 2 + len(rr)
     V.wait_ge(S.jot, 2)
     vi(V.tensor_scalar(T.J2[:], T.J0[:], 15, None, A.bitwise_and))
     vw()
     vi(V.tensor_tensor(T.JJ[:], T.J2[:], T.J1[:], A.add))
+    vw()
+    vi(V.tensor_scalar(T.JL[:], T.JJ[:, 0:LC], 1.0 / LO, None, A.mult))
+    vi(V.tensor_scalar(T.JO[:], T.JJ[:], 1.0 / PO, None, A.mult))
 
     def quant(dst, b, src, a, cols):
         return V.quantize_mx(T[dst + "c"][:, b:b + cols], T[dst + "s"][:, b:b + cols], src[:, 4 * a:4 * (a + cols)])
@@ -296,34 +322,13 @@ def rank_program(g, core, T, topo):
     w8 = LC * nr
     V.wait_ge(S.kp, total[core, "kp"])
     vw()
-    vi(V.tensor_tensor(T.o1[:, 0:w8], T.KL[:, LC:LC + w8], T.KO[:, LC:LC + w8], A.is_gt))
-    vi(V.tensor_tensor(T.cm[:, 0:LC + w8], T.KL[:, 0:LC + w8], T.KO[:, 0:LC + w8], A.max))
+    vi(V.tensor_tensor(T.o1[:, 0:LC], T.KL[:, 1:2 * LC:2], T.KO[:, 1:2 * LC:2], A.is_gt))
+    vi(V.tensor_tensor(T.o1[:, LC:w8], T.KL[:, 2 * LC:LC + w8], T.KO[:, 2 * LC:LC + w8], A.is_gt))
+    vi(V.tensor_tensor(T.cm[:], T.KL[:, 0:2 * LC], T.KO[:, 0:2 * LC], A.max))
     vw()
-    vi(V.tensor_scalar(T.o2[:, 0:w8], T.o1[:, 0:w8], LO * nr, None, A.mult))
+    vi(V.tensor_tensor(T.o2[:, 0:w8], T.o1[:, 0:w8], T.JO[:, 0:w8], A.add))
     vw()
-    vi(V.tensor_tensor(T.o3[:, 0:w8], T.o2[:, 0:w8], T.JJ[:, 0:w8], A.add))
-    vw()
-    V.tensor_copy(T.lo[:, 0:w8], T.o3[:, 0:w8]).then_inc(S.llo, 1)
-    V.wait_ge(S.kl, total[core, "kl"])
-    vi(V.tensor_tensor(T.ab[:], T.KW[:, 0:32], T.KW[:, 32:64], A.max))
-    vw()
-    vi(V.tensor_tensor(T.m1[:], T.cm[:, 0:LC], T.ab[:, 0:LC], A.max))
-    vi(V.tensor_tensor(T.n1[:], T.cm[:, w8:LC + w8], T.ab[:, LC:2 * LC], A.max))
-    vw()
-    V.tensor_tensor(T.PM[:], T.m1[:], T.ab[:, 2 * LC:3 * LC], A.max).then_inc(S.pm, 1)
-    vi(V.tensor_tensor(T.om[:], T.n1[:], T.ab[:, 3 * LC:4 * LC], A.max))
-    V.wait_ge(S.pm, 1)
-    vw()
-    vi(V.tensor_scalar(T.p1[:], T.PM[:], LOW - 1, None, A.bitwise_and))
-    vi(V.tensor_scalar(T.f1[:], T.om[:], LOW - 1, 1, A.bitwise_and, A.logical_shift_right))
-    vi(V.tensor_scalar(T.f2[:], T.om[:], 3, None, A.logical_shift_right))
-    vw()
-    vi(V.tensor_scalar(T.p2[:], T.p1[:], LO, -2 * LO, A.mult, A.add))
-    vi(V.tensor_scalar(T.f3[:], T.f1[:], LO, None, A.mult))
-    vw()
-    vi(V.tensor_tensor(T.p3[:], T.p2[:], T.JJ[:, 0:LC], A.add))
-    vw()
-    V.tensor_copy(T.lp[:], T.p3[:]).then_inc(S.llp, 1)
+    V.tensor_scalar(T.lo[:, 0:w8], T.o2[:, 0:w8], PO, None, A.mult).then_inc(S.llo, 1)
     V.wait_ge(S.wl, 16)
     quant("WQ", 0, T.BW, 0, LO).then_inc(S.wq, 1)
 
@@ -338,22 +343,41 @@ def rank_program(g, core, T, topo):
     slot = LO * (3 - f["ci"])
     V.wait_ge(S.llo, 1)
     V.wait_ge(S.oec, total[core, "oec"])
-    if nr > 1:
-        pick_c("SO", 0, "WO", 2 * LO * nr, "lo", 0, LC * (nr - 1)).then_inc(S.pko, 1)
-    vi(pick_c("WF", slot, "WO", 2 * LO * nr, "lo", LC * (nr - 1), LC))
+    pick_c("SO", 0, "WO", PO + LO * nr, "lo", LC, LC * (nr - 1)).then_inc(S.pko, 1)
+    vi(pick_c("WF", slot, "WO", PO + LO * nr, "lo", 0, LC))
+    V.wait_ge(S.kl, total[core, "kl"])
+    vi(V.tensor_tensor(T.ab[:], T.KW[:, 0:32], T.KW[:, 32:64], A.max))
+    vw()
+    vi(V.tensor_tensor(T.m1[:], T.cm[:], T.ab[:, 0:16], A.max))
+    vw()
+    V.tensor_tensor(T.PM[:], T.m1[:, 0:16:2], T.ab[:, 16:32:2], A.max).then_inc(S.pm, 1)
+    V.wait_ge(S.pm, 1)
+    vi(V.tensor_scalar(T.p1[:], T.PM[:], LOW - 1, None, A.bitwise_and))
+    vi(V.tensor_tensor(T.om[:], T.m1[:, 1:16:2], T.ab[:, 17:32:2], A.max))
+    vw()
+    vi(V.tensor_tensor(T.p2[:], T.p1[:], T.JL[:], A.add))
+    vi(V.tensor_scalar(T.f1[:], T.om[:], LOW - 1, None, A.bitwise_and))
+    vi(V.tensor_scalar(T.f3[:], T.om[:], LOW - 1, 1, A.bitwise_and, A.logical_shift_right))
+    vw()
+    V.tensor_scalar(T.lp[:], T.p2[:], LO, -2 * LO, A.mult, A.add).then_inc(S.llp, 1)
+    vi(V.tensor_tensor(T.f2[:], T.om[:], T.f1[:], A.subtract))
+    own = T.f2
+    if f["h"] == 0:
+        vw()
+        vi(V.tensor_scalar(T.f4[:], T.f2[:], LOW, None, A.add))
+        own = T.f4
     V.wait_ge(S.llp, 1)
     V.wait_ge(S.pac, total[core, "pac"])
     pick_c("XP", 0, "WP", 6 * LO, "lp", 0, LC).then_inc(S.xpc, 1)
     V.wait_ge(S.kx, total[core, "kx"])
-    vi(V.tensor_scalar(T.f4[:], T.KX[:], 3, None, A.logical_shift_right))
     vw()
-    vi(V.tensor_tensor(T.f5[:], T.f2[:], T.f4[:], A.is_ge if f["h"] == 0 else A.is_gt))
+    vi(V.tensor_tensor(T.f5[:], own[:], T.KX[:], A.is_gt))
     vw()
     vi(V.tensor_tensor(T.f6[:], T.f5[:], T.f3[:], A.mult))
     vw()
-    vi(V.tensor_tensor(T.f7[:], T.f6[:], T.JJ[:, 0:LC], A.add))
+    vi(V.tensor_tensor(T.f7[:], T.f6[:], T.JL[:], A.add))
     vw()
-    V.tensor_copy(T.lf[:], T.f7[:]).then_inc(S.llf, 1)
+    V.tensor_scalar(T.lf[:], T.f7[:], LO, None, A.mult).then_inc(S.llf, 1)
     V.wait_ge(S.llf, 1)
     V.wait_ge(S.ogc, total[core, "ogc"])
     V.wait_ge(S.xxc, total[core, "xxc"])
@@ -361,12 +385,10 @@ def rank_program(g, core, T, topo):
     V.wait_ge(S.mm, 1)
     V.tensor_copy(T.ys[:], T.ps[:, 0:LO]).then_inc(S.yc, 1)
 
-    ns = [0]
     ACT.wait_ge(S.llo, 1)
     ACT.wait_ge(S.oes, total[core, "oes"])
-    if nr > 1:
-        pick_s("SO", 0, "WO", 2 * LO * nr, "lo", 0, LC * (nr - 1)).then_inc(S.pks, 1)
-    pick_s("WF", slot, "WO", 2 * LO * nr, "lo", LC * (nr - 1), LC).then_inc(S.s, 1)
+    pick_s("SO", 0, "WO", PO + LO * nr, "lo", LC, LC * (nr - 1)).then_inc(S.pks, 1)
+    pick_s("WF", slot, "WO", PO + LO * nr, "lo", 0, LC).then_inc(S.s, 1)
     ACT.wait_ge(S.llp, 1)
     ACT.wait_ge(S.pas, total[core, "pas"])
     pick_s("XP", 0, "WP", 6 * LO, "lp", 0, LC).then_inc(S.xps, 1)
@@ -388,8 +410,9 @@ def rank_program(g, core, T, topo):
     def send(label):
         issue(g, core, T, topo, my[label])
 
-    g.wait_ge(S.kk, nk)
-    send("key")
+    g.wait_ge(S.ks, 4)
+    g.wait_ge(S.kk, npk)
+    send("k1")
     for n, k in enumerate(f["others"]):
         if k in f["relay"]:
             g.wait_ge(S["qp%d" % n], 1)
@@ -402,16 +425,17 @@ def rank_program(g, core, T, topo):
     g.wait_ge(S.qp2, 1)
     send("pdc")
     send("pds")
+    if "k2" in my:
+        send("k2")
     g.wait_ge(S.qo, nqo)
     send("oec")
     send("oes")
+    g.wait_ge(S.pko, 1)
+    send("ogc")
+    g.wait_ge(S.pks, 1)
+    send("ogs")
     g.wait_ge(S.pm, 1)
     send("kx")
-    if nr > 1:
-        g.wait_ge(S.pko, 1)
-        send("ogc")
-        g.wait_ge(S.pks, 1)
-        send("ogs")
     g.wait_ge(S.xpc, 1)
     send("xxc")
     g.wait_ge(S.xps, 1)

from concourse.bass import DstId, RemoteDMATransfer
from concourse.mybir import dt, AluOpType, ActivationFunctionType

LO = 128
LC = 8
LOW = 8
PO = 512

F8, U8, I32, U16, BF, F32 = "float8_e4m3fn_x4", "uint8", "int32", "uint16", "bfloat16", "float32"
PAIRS = {"QP": 640, "WP": 768, "XP": 128,
         "QO": 640, "WO": 1024, "SO": 384,
         "WF": 512, "MF": 128, "WQ": 128,
         "RP": 256, "RO": 128}
SCRATCH = {
    "BP": ("sbuf", [128, 3072], BF), "BO": ("sbuf", [128, 3072], BF), "BW": ("sbuf", [128, 512], BF),
    "SC": ("sbuf", [128, 96], I32), "KS": ("sbuf", [128, 64], I32), "KP": ("sbuf", [128, 40], I32),
    "KO": ("sbuf", [128, 40], I32), "KL": ("sbuf", [128, 40], I32), "KW": ("sbuf", [128, 64], I32),
    "KX": ("sbuf", [128, LC], I32), "RK": ("sbuf", [128, 32], I32), "PM": ("sbuf", [128, LC], I32),
    "J0": ("sbuf", [128, 32], I32), "J1": ("sbuf", [128, 32], I32), "J2": ("sbuf", [128, 32], I32),
    "JJ": ("sbuf", [128, 32], I32), "JL": ("sbuf", [128, LC], F32), "JO": ("sbuf", [128, 32], F32),
    "o1": ("sbuf", [128, 32], I32), "o2": ("sbuf", [128, 32], F32),
    "cm": ("sbuf", [128, 16], I32), "ab": ("sbuf", [128, 32], I32), "m1": ("sbuf", [128, 16], I32),
    "om": ("sbuf", [128, LC], I32), "p1": ("sbuf", [128, LC], I32), "p2": ("sbuf", [128, LC], F32),
    "f1": ("sbuf", [128, LC], I32), "f2": ("sbuf", [128, LC], I32), "f3": ("sbuf", [128, LC], I32),
    "f4": ("sbuf", [128, LC], I32), "f5": ("sbuf", [128, LC], I32), "f6": ("sbuf", [128, LC], I32),
    "f7": ("sbuf", [128, LC], F32),
    "lo": ("sbuf", [128, 32], U16), "lp": ("sbuf", [128, LC], U16), "lf": ("sbuf", [128, LC], U16),
    "ps": ("psum", [128, 512], F32), "ys": ("sbuf", [128, LO], F32),
}
for _n, _w in PAIRS.items():
    SCRATCH[_n + "c"] = ("sbuf", [128, _w], F8)
    SCRATCH[_n + "s"] = ("sbuf", [128, _w], U8)
SEMAPHORES = ["xl0", "xl1", "xl2", "xl3", "xl4", "xl5", "wl", "scl", "jot", "ks", "kk", "v", "s", "qp0", "qp1", "qp2", "qo",
              "wq", "kp", "kl", "kx", "pac", "pas", "oec", "oes", "ogc", "ogs", "xxc", "xxs", "hk", "hpc", "hps", "hoc",
              "hos", "ls", "llo", "llp", "llf", "pm", "pko", "pks", "xpc", "xps", "mfc", "mfs", "mm", "yc", "yst"]


def runs(pairs, width):
    out = []
    for a, b in pairs:
        if out and out[-1][0] + out[-1][2] == a and out[-1][1] + out[-1][2] == b:
            out[-1][2] += width
        else:
            out.append([a, b, width])
    return out


def ranks_info(T, topo):
    cores = [int(c) for c in T.cores]
    hosts = sorted(set(topo.host(c) for c in cores))
    by = [[c for c in cores if topo.host(c) == h] for h in hosts]
    info = {}
    for h, cs in enumerate(by):
        groups = []
        for c in cs:
            if groups and topo.chip(groups[-1][0]) == topo.chip(c):
                groups[-1].append(c)
            else:
                groups.append([c])
        for ci, grp in enumerate(groups):
            able = {}
            for k, G in enumerate(groups):
                if k != ci:
                    able[k] = [c for c in grp if all(topo.may_write(c, d) for d in G)]
            makes = {c: [] for c in grp}
            for k in sorted(able, key=lambda k: len(able[k])):
                c = min(able[k], key=lambda c: len(makes[c]))
                makes[c] += groups[k]
            if any(not makes[c] for c in grp):
                makes = {c: [groups[k][m] for k in sorted(able)] for m, c in enumerate(grp)}
            for c in grp:
                others = [k for k in range(len(groups)) if k != ci]
                direct = {k: all(topo.may_write(c, d) for d in groups[k]) for k in others}
                others.sort(key=lambda k: (direct[k], k))
                relay = {}
                for k in others:
                    if not direct[k]:
                        hs = [m for m in topo.cores_of(c) if m not in cores and topo.die(m) == topo.die(c)
                              and all(topo.may_write(m, d) for d in groups[k])]
                        relay[k] = hs[len(relay) % len(hs)]
                info[c] = {"h": h, "i": cs.index(c), "ci": ci, "groups": groups, "others": others, "relay": relay,
                           "partner": [d for d in grp if d != c][0], "twin": by[1 - h][cs.index(c)],
                           "R": [c] + makes[c], "rank": cores.index(c)}
    return info


def key_slot(info, d, s):
    a = sorted(info[d]["others"]).index(info[s]["ci"])
    k = info[d]["groups"][info[s]["ci"]].index(s)
    return 2 * LC * (2 * k + a)


def deal(topo, src, dsts, on_only):
    chip = topo.cores_of(src)
    off = [d for d in dsts if d not in chip]
    on = [d for d in dsts if d in chip]
    pools = {}
    if off:
        pools[True] = [e for e in topo.engines(src, off[0]) if all(e in topo.engines(src, d) for d in off)]
    if on:
        pools[False] = [e for e in topo.engines(src, on[0]) if e not in (pools.get(True) or on_only)]
    res, used = [], {True: 0, False: 0}
    for d in dsts:
        o = d not in chip
        n = len(off) if o else len(on)
        w = 1
        while 2 * w * n <= len(pools[o]):
            w *= 2
        res.append(pools[o][used[o]:used[o] + w])
        used[o] += w
    return res


def make_calls(T, topo, info):
    calls = {}

    def add(core, label, transfers, on_only=()):
        by = {}
        for t in transfers:
            by.setdefault(t[5], []).append(t)
        for w in by:
            es = deal(topo, core, [t[0] for t in by[w]], on_only)
            calls.setdefault(core, {}).setdefault(label, []).append([t + (e,) for t, e in zip(by[w], es)])

    for c, f in info.items():
        p, G = f["partner"], f["groups"]
        nr = len(info[p]["R"])
        offs = topo.engines(c, f["twin"]) if len(f["relay"]) < len(f["others"]) else []
        tr, dr = [], []
        for n, k in enumerate(f["others"]):
            if k in f["relay"]:
                hcore = f["relay"][k]
                tr.append((hcore, "KS", 32 * n, "RK", 0, 32, "hk"))
                add(hcore, "key", [(d, "RK", 16 * m, "KW", key_slot(info, d, c), 16, "kl") for m, d in enumerate(G[k])])
            else:
                dr += [(d, "KS", 32 * n + 16 * m, "KW", key_slot(info, d, c), 16, "kl") for m, d in enumerate(G[k])]
        kp = [(p, "KP", 0, "KL", 0, LC * (1 + nr), "kp")]
        if tr:
            add(c, "k1", tr + kp)
            if dr:
                add(c, "k2", dr)
        else:
            add(c, "k1", dr)
            add(c, "k2", kp, offs)
        for q in "cs":
            slot = LO * (5 - f["i"])
            tr = []
            for n, k in enumerate(f["others"]):
                if k in f["relay"]:
                    hcore = f["relay"][k]
                    tr.append((hcore, "QP" + q, 256 * n, "RP" + q, 0, 256, "hp" + q))
                    add(hcore, "p" + q, [(d, "RP" + q, LO * m, "WP" + q, slot, LO, "pa" + q) for m, d in enumerate(G[k])])
            if tr:
                add(c, "pr" + q, tr)
            tr = []
            for n, k in enumerate(f["others"]):
                if k not in f["relay"]:
                    tr += [(d, "QP" + q, 256 * n + LO * m, "WP" + q, slot, LO, "pa" + q) for m, d in enumerate(G[k])]
            tr.append((p, "QP" + q, 512, "WP" + q, slot, LO, "pa" + q))
            add(c, "pd" + q, tr)
            add(c, "oe" + q, [(p, "QO" + q, 0, "WO" + q, PO, LO * nr, "oe" + q)], offs)
            tr, slot = [], LO * (3 - f["ci"])
            for n, d in enumerate(f["R"][1:]):
                hcore = f["relay"].get(info[d]["ci"])
                if hcore is None:
                    tr.append((d, "SO" + q, LO * n, "WF" + q, slot, LO, "og" + q))
                else:
                    tr.append((hcore, "SO" + q, LO * n, "RO" + q, 0, LO, "ho" + q))
                    add(hcore, "o" + q, [(d, "RO" + q, 0, "WF" + q, slot, LO, "og" + q)])
            add(c, "og" + q, tr)
            add(c, "xx" + q, [(f["twin"], "XP" + q, 0, "WF" + q, 0, LO, "xx" + q)])
        add(c, "kx", [(f["twin"], "PM", 0, "KX", 0, LC, "kx")])
    total = {}
    for c in calls:
        for label in calls[c]:
            for call in calls[c][label]:
                for t in call:
                    total[t[0], t[6]] = total.get((t[0], t[6]), 0) + len(t[7])
                    total[c, "ls"] = total.get((c, "ls"), 0) + len(t[7])
    return calls, total


CACHE = {}


def view(T, name, a, w):
    ap = T[name][:, a:a + w]
    return ap.bitcast(dt.uint8) if SCRATCH[name][2] == F8 else ap


def issue(g, core, T, topo, calls):
    for call in calls:
        trs = []
        for dst, sb, a, db, b, w, sem, eng in call:
            rid, pid = topo.addr(dst, core)
            mask = sum(1 << e for e in eng)
            trs.append((view(T, db, b, w), view(T, sb, a, w), T.sem[sem], rid, pid, mask))
        if len(trs) == 1:
            o, i, sem, rid, pid, mask = trs[0]
            g.remote_dma(o, i, sem, T.sem.ls, pid, rid, mask)
        else:
            g.remote_dma_fused([RemoteDMATransfer(dst_ids=[DstId(rid=rid, pnc=pid)], dma_engine_mask=mask, remote_sem=sem,
                                                  src=i, dst=o) for o, i, sem, rid, pid, mask in trs], local_sem=T.sem.ls)


def forward_program(g, core, T, topo, calls, total):
    for label, sem in (("key", "hk"), ("pc", "hpc"), ("ps", "hps"), ("oc", "hoc"), ("os", "hos")):
        if label in calls:
            g.wait_ge(T.sem[sem], total[core, sem])
            issue(g, core, T, topo, calls[label])
    g.wait_ge(T.sem.ls, total[core, "ls"])


def rank_program(g, core, T, topo):
    if "plan" not in CACHE:
        CACHE["info"] = ranks_info(T, topo)
        CACHE["plan"] = make_calls(T, topo, CACHE["info"])
    info, (calls, total) = CACHE["info"], CACHE["plan"]
    if core not in calls:
        return
    if core not in info:
        forward_program(g, core, T, topo, calls[core], total)
        return
    my, f = calls[core], info[core]
    S, A = T.sem, AluOpType
    V, ACT = g.vector, g.scalar
    p, G, R = f["partner"], f["groups"], f["R"]
    RP = info[p]["R"]
    nr = len(R)
    grp = G[f["ci"]]
    own_o = lambda d: info[d]["rank"]
    own_p = lambda d: info[info[d]["twin"]]["rank"]

    pchunks = f["others"] + [f["ci"]]
    ochunks = sorted(range(len(G)), key=lambda k: (0 if any(d in RP for d in G[k] if d != p) else 1 if k == f["ci"] else 2))

    def load_x(q, n):
        k = (pchunks + ochunks)[n]
        first = (own_p if n < 3 else own_o)(G[k][0])
        buf = T.BP if n < 3 else T.BO
        q.dma_start(buf[:, 1024 * (n % 3):1024 * (n % 3) + 1024], T.x[:, 512 * first:512 * first + 1024]).then_inc(S["xl%d" % n], 16)

    def load_sc(q, t):
        q.dma_start(T.SC[16 * t:16 * t + 16, :], T.sc[:, :]).then_inc(S.scl, 16)

    load_x(g.sync, 0)
    for t in range(5, 8):
        load_sc(g.sync, t)
    for n in (1, 3, 5):
        load_x(g.sync, n)
    for t in range(5):
        load_sc(ACT, t)
    for n in (2, 4):
        load_x(ACT, n)
    g.sync.dma_start(T.BW[:], T.w[:, :]).then_inc(S.wl, 16)

    g.iota(T.J0[:], [[0, 32]], 0, 1).then_inc(S.jot, 1)
    g.iota(T.J1[:], [[16, 32]], 0, 0).then_inc(S.jot, 1)

    nv = [0]

    def vi(ins):
        ins.then_inc(S.v, 1)
        nv[0] += 1

    def vw():
        V.wait_ge(S.v, nv[0])

    V.wait_ge(S.scl, 128)
    low = LOW - 1 - f["i"]

    def key(buf, b, e, step, a, sem):
        w = len(range(b, e, step))
        ins = V.tensor_scalar(buf[:, b:e:step], T.SC[:, a:a + w], LOW, low, A.mult, A.add)
        if sem is None:
            vi(ins)
        else:
            ins.then_inc(sem, 1)

    for n, k in enumerate(f["others"]):
        b = 4 * LC * n
        key(T.KS, b, b + 4 * LC, 2, LC * own_p(G[k][0]), S.ks)
        key(T.KS, b + 1, b + 4 * LC, 2, LC * own_o(G[k][0]), S.ks)
    npk = 0
    for buf, lst, sem in ((T.KP, RP, S.kk), (T.KO, R, None)):
        key(buf, 0, 2 * LC, 2, LC * own_p(lst[0]), sem)
        key(buf, 1, 2 * LC, 2, LC * own_o(lst[0]), sem)
        rr = runs([(LC * own_o(d), LC * (1 + n)) for n, d in enumerate(lst) if n], LC)
        for a, b, w in rr:
            key(buf, b, b + w, 1, a, sem)
        npk = npk or 2 + len(rr)
    V.wait_ge(S.jot, 2)
    vi(V.tensor_scalar(T.J2[:], T.J0[:], 15, None, A.bitwise_and))
    vw()
    vi(V.tensor_tensor(T.JJ[:], T.J2[:], T.J1[:], A.add))
    vw()
    vi(V.tensor_scalar(T.JL[:], T.JJ[:, 0:LC], 1.0 / LO, None, A.mult))
    vi(V.tensor_scalar(T.JO[:], T.JJ[:], 1.0 / PO, None, A.mult))

    def quant(dst, b, src, a, cols):
        return V.quantize_mx(T[dst + "c"][:, b:b + cols], T[dst + "s"][:, b:b + cols], src[:, 4 * a:4 * (a + cols)])

    for n in (0, 1):
        V.wait_ge(S["xl%d" % n], 16)
        quant("QP", 256 * n, T.BP, 256 * n, 256).then_inc(S["qp%d" % n], 1)
    V.wait_ge(S.xl2, 16)
    quant("QP", 512, T.BP, 512 + LO * grp.index(p), LO).then_inc(S.qp2, 1)
    vi(quant("WP", LO * (5 - f["i"]), T.BP, 512 + LO * grp.index(core), LO))
    nqo = 0
    for n in range(3):
        V.wait_ge(S["xl%d" % (3 + n)], 16)
        k = ochunks[n]
        for lst, dst in ((RP, "QO"), (R, "WO")):
            for a, b, w in runs([(256 * n + LO * m, LO * lst.index(d)) for m, d in enumerate(G[k]) if d in lst], LO):
                ins = quant(dst, b, T.BO, a, w)
                if dst == "QO":
                    ins.then_inc(S.qo, 1)
                    nqo += 1
                else:
                    vi(ins)

    w8 = LC * nr
    V.wait_ge(S.kp, total[core, "kp"])
    vw()
    vi(V.tensor_tensor(T.o1[:, 0:LC], T.KL[:, 1:2 * LC:2], T.KO[:, 1:2 * LC:2], A.is_gt))
    vi(V.tensor_tensor(T.o1[:, LC:w8], T.KL[:, 2 * LC:LC + w8], T.KO[:, 2 * LC:LC + w8], A.is_gt))
    vi(V.tensor_tensor(T.cm[:], T.KL[:, 0:2 * LC], T.KO[:, 0:2 * LC], A.max))
    vw()
    vi(V.tensor_tensor(T.o2[:, 0:w8], T.o1[:, 0:w8], T.JO[:, 0:w8], A.add))
    vw()
    V.tensor_scalar(T.lo[:, 0:w8], T.o2[:, 0:w8], PO, None, A.mult).then_inc(S.llo, 1)
    V.wait_ge(S.wl, 16)
    quant("WQ", 0, T.BW, 0, LO).then_inc(S.wq, 1)

    def pick_c(dst, b, src, w, lst, a, k):
        return V.tensor_copy(T[dst + "c"][:, b:b + LC * 2 * k].bitcast(dt.uint32),
                             T[src + "c"][:, 0:w].bitcast(dt.uint32).indirect(T[lst][:, a:a + k]))

    def pick_s(dst, b, src, w, lst, a, k):
        return ACT.activation(T[dst + "s"][:, b:b + LC * 2 * k], T[src + "s"][:, 0:w].indirect(T[lst][:, a:a + k]),
                              ActivationFunctionType.Copy)

    slot = LO * (3 - f["ci"])
    V.wait_ge(S.llo, 1)
    V.wait_ge(S.oec, total[core, "oec"])
    pick_c("SO", 0, "WO", PO + LO * nr, "lo", LC, LC * (nr - 1)).then_inc(S.pko, 1)
    vi(pick_c("WF", slot, "WO", PO + LO * nr, "lo", 0, LC))
    V.wait_ge(S.kl, total[core, "kl"])
    vi(V.tensor_tensor(T.ab[:], T.KW[:, 0:32], T.KW[:, 32:64], A.max))
    vw()
    vi(V.tensor_tensor(T.m1[:], T.cm[:], T.ab[:, 0:16], A.max))
    vw()
    V.tensor_tensor(T.PM[:], T.m1[:, 0:16:2], T.ab[:, 16:32:2], A.max).then_inc(S.pm, 1)
    V.wait_ge(S.pm, 1)
    vi(V.tensor_scalar(T.p1[:], T.PM[:], LOW - 1, None, A.bitwise_and))
    vi(V.tensor_tensor(T.om[:], T.m1[:, 1:16:2], T.ab[:, 17:32:2], A.max))
    vw()
    vi(V.tensor_tensor(T.p2[:], T.p1[:], T.JL[:], A.add))
    vi(V.tensor_scalar(T.f1[:], T.om[:], LOW - 1, None, A.bitwise_and))
    vi(V.tensor_scalar(T.f3[:], T.om[:], LOW - 1, 1, A.bitwise_and, A.logical_shift_right))
    vw()
    V.tensor_scalar(T.lp[:], T.p2[:], LO, -2 * LO, A.mult, A.add).then_inc(S.llp, 1)
    vi(V.tensor_tensor(T.f2[:], T.om[:], T.f1[:], A.subtract))
    own = T.f2
    if f["h"] == 0:
        vw()
        vi(V.tensor_scalar(T.f4[:], T.f2[:], LOW, None, A.add))
        own = T.f4
    V.wait_ge(S.llp, 1)
    V.wait_ge(S.pac, total[core, "pac"])
    pick_c("XP", 0, "WP", 6 * LO, "lp", 0, LC).then_inc(S.xpc, 1)
    V.wait_ge(S.kx, total[core, "kx"])
    vw()
    vi(V.tensor_tensor(T.f5[:], own[:], T.KX[:], A.is_gt))
    vw()
    vi(V.tensor_tensor(T.f6[:], T.f5[:], T.f3[:], A.mult))
    vw()
    vi(V.tensor_tensor(T.f7[:], T.f6[:], T.JL[:], A.add))
    vw()
    V.tensor_scalar(T.lf[:], T.f7[:], LO, None, A.mult).then_inc(S.llf, 1)
    V.wait_ge(S.llf, 1)
    V.wait_ge(S.ogc, total[core, "ogc"])
    V.wait_ge(S.xxc, total[core, "xxc"])
    pick_c("MF", 0, "WF", 4 * LO, "lf", 0, LC).then_inc(S.mfc, 1)
    V.wait_ge(S.mm, 1)
    V.tensor_copy(T.ys[:], T.ps[:, 0:LO]).then_inc(S.yc, 1)

    ACT.wait_ge(S.llo, 1)
    ACT.wait_ge(S.oes, total[core, "oes"])
    pick_s("SO", 0, "WO", PO + LO * nr, "lo", LC, LC * (nr - 1)).then_inc(S.pks, 1)
    pick_s("WF", slot, "WO", PO + LO * nr, "lo", 0, LC).then_inc(S.s, 1)
    ACT.wait_ge(S.llp, 1)
    ACT.wait_ge(S.pas, total[core, "pas"])
    pick_s("XP", 0, "WP", 6 * LO, "lp", 0, LC).then_inc(S.xps, 1)
    ACT.wait_ge(S.llf, 1)
    ACT.wait_ge(S.s, 1)
    ACT.wait_ge(S.ogs, total[core, "ogs"])
    ACT.wait_ge(S.xxs, total[core, "xxs"])
    pick_s("MF", 0, "WF", 4 * LO, "lf", 0, LC).then_inc(S.mfs, 1)

    g.tensor.wait_ge(S.wq, 1)
    g.tensor.wait_ge(S.mfs, 1)
    g.tensor.wait_ge(S.mfc, 1)
    g.tensor.matmul_mx(T.ps[:, 0:LO], T.WQc[:, 0:LO], T.WQs[:, 0:LO], T.MFc[:, 0:LO], T.MFs[:, 0:LO], True, True).then_inc(S.mm, 1)
    g.sync.wait_ge(S.yc, 1)
    g.sync.dma_start(T.y[:, :], T.ys[:]).then_inc(S.yst, 16)
    g.sync.wait_ge(S.yst, 16)
    V.wait_ge(S.v, nv[0])

    def send(label):
        issue(g, core, T, topo, my[label])

    g.wait_ge(S.ks, 4)
    g.wait_ge(S.kk, npk)
    send("k1")
    for n, k in enumerate(f["others"]):
        if k in f["relay"]:
            g.wait_ge(S["qp%d" % n], 1)
    if f["relay"]:
        send("prc")
        send("prs")
    for n, k in enumerate(f["others"]):
        if k not in f["relay"]:
            g.wait_ge(S["qp%d" % n], 1)
    g.wait_ge(S.qp2, 1)
    send("pdc")
    send("pds")
    if "k2" in my:
        send("k2")
    g.wait_ge(S.qo, nqo)
    send("oec")
    send("oes")
    g.wait_ge(S.pko, 1)
    send("ogc")
    g.wait_ge(S.pks, 1)
    send("ogs")
    g.wait_ge(S.pm, 1)
    send("kx")
    g.wait_ge(S.xpc, 1)
    send("xxc")
    g.wait_ge(S.xps, 1)
    send("xxs")
    g.wait_ge(S.ls, total[core, "ls"])
